import numpy as np
import ml_dtypes


def mxq(x, axis, fmt="e4m3"):
    dtype, down = {"e4m3": (ml_dtypes.float8_e4m3fn, 7), "e5m2": (ml_dtypes.float8_e5m2, 14)}[fmt]
    v = np.moveaxis(np.asarray(x, np.float32).astype(ml_dtypes.bfloat16).astype(np.float64), axis, -1)
    blocks = v.reshape(v.shape[:-1] + (-1, 32))
    amax = np.abs(blocks).max(-1, keepdims=True)
    byte = np.maximum(np.where(amax > 0, np.frexp(amax)[1] - 1 + 127, 0) - down, 1)
    scale = np.exp2(byte - 127.0)
    codes = (blocks / scale).astype(np.float32).astype(dtype).astype(np.float64)
    return np.moveaxis((codes * scale).reshape(v.shape), -1, axis)


WIDE = False


def mx_kscale(k):
    if not WIDE:
        return np.ones(k)
    levels = np.array([10, -10, 5, -5, 0])
    if k % 512:
        return np.exp2(np.random.permutation(np.resize(levels, k // 32))).repeat(32)
    a = np.empty((k // 512, 16))
    for p in range(k // 512):
        a[p, :8] = np.random.permutation(np.resize(levels, 8))
        for g in range(8):
            far = levels[np.abs(levels - a[p, g]) >= 10]
            a[p, g + 8] = far[np.random.randint(len(far))]
    return np.exp2(a.ravel()).repeat(32)


def f64(x):
    return np.asarray(x).astype(np.float64)


def striped(idx):
    return np.tile(idx.reshape(-1, 16).T, (8, 1)).astype(np.uint16)


def unstriped(offs):
    return offs[:16].T.reshape(-1).astype(np.int64)


E2M1 = np.array([0.0, 0.5, 1.0, 1.5, 2.0, 3.0, 4.0, 6.0, -0.0, -0.5, -1.0, -1.5, -2.0, -3.0, -4.0, -6.0])


def pack_weight(w, fmt):
    k, n = w.shape
    w = f64(np.asarray(w, np.float32).astype(ml_dtypes.bfloat16)).reshape(k // 32, 32, n)
    amax = np.abs(w).max(1)
    if fmt == "e4m3":
        byte = np.frexp(amax)[1] - 1 + 127 - 7
    else:
        mant, ex = np.frexp(amax / 6.0)
        byte = np.where(mant > 0.5, ex, ex - 1) + 127
    byte = np.clip(np.where(amax > 0, byte, 1), 1, 254)
    scaled = (w * np.exp2(127.0 - byte)[:, None, :]).reshape(k, n).astype(np.float32)
    by_word = np.ascontiguousarray(scaled.reshape(k // 512, 128, 4, n).transpose(0, 1, 3, 2))
    if fmt == "e4m3":
        words = by_word.astype(ml_dtypes.float8_e4m3fn).view(np.uint8)
    else:
        c = by_word.astype(ml_dtypes.float4_e2m1fn).view(np.uint8) & 0xF
        words = (c[..., 0::2] | (c[..., 1::2] << 4)).reshape(k // 512, 128, 2 * n)
    return np.ascontiguousarray(words), np.ascontiguousarray(byte.astype(np.uint8).reshape(k // 512, 16, n))


def unpack_weight(words, scales, fmt):
    g, _, n = scales.shape
    words = np.ascontiguousarray(words).reshape(g, 128, n, -1)
    if fmt == "e4m3":
        vals = words.view(ml_dtypes.float8_e4m3fn).astype(np.float64)
    else:
        nib = np.empty((g, 128, n, 4), np.uint8)
        nib[..., 0::2] = words & 0xF
        nib[..., 1::2] = words >> 4
        vals = E2M1[nib]
    vals = vals * np.repeat(np.exp2(scales.astype(np.float64) - 127.0), 8, axis=1)[..., None]
    return vals.transpose(0, 1, 3, 2).reshape(g * 512, n)


def gelu(v):
    return 0.5 * v * (1.0 + np.tanh(np.sqrt(2.0 / np.pi) * (v + 0.044715 * v**3)))


def often(T, S):
    return np.random.permutation(T)[(T * np.random.uniform(0, 1, S) ** 4).astype(np.int64)]


K, M, T, S, P, H, N = 1024, 512, 4096, 1024, 512, 1024, 512


def setup_inputs():
    n = np.random.standard_normal
    s = mx_kscale(K)[:, None]
    s2 = mx_kscale(M)[:, None]
    u = mx_kscale(H)[:, None]
    d = {}
    d["tab_words"], d["tab_scales"] = pack_weight(n((K, T)) * s, "e4m3")
    d["tab2_words"], d["tab2_scales"] = pack_weight(n((M, T)) * s2, "e4m3")
    d["tab3_words"], d["tab3_scales"] = pack_weight(n((M, T)) * s2, "e4m3")
    d["offs"] = striped(np.random.permutation(T)[:S])
    d["offs2"] = striped(np.random.permutation(T)[:S])
    d["offs3"] = striped(np.random.permutation(T)[:S])
    d["pos1"] = striped(np.random.permutation(S)[:P])
    d["pos2"] = striped(often(S, P))
    d["pos3"] = striped(often(S, P))
    d["wa"] = (1.5 * n((K, H)) / K ** 0.5 / s).astype(np.float32)
    d["wb_words"], d["wb_scales"] = pack_weight(n((M, H)) / M ** 0.5 / s2 * u.T, "e2m1")
    d["wd"] = (n((M, H)) / M ** 0.5 / s2 * u.T).astype(np.float32)
    d["wo_words"], d["wo_scales"] = pack_weight(1.5 * n((H, N)) / H ** 0.5 / u, "e4m3")
    d["style"] = (0.7 * n(N)).astype(np.float32)
    return d


def reference(tab_words, tab_scales, tab2_words, tab2_scales, tab3_words, tab3_scales, offs, offs2, offs3,
              pos1, pos2, pos3, wa, wb_words, wb_scales, wd, wo_words, wo_scales, style):
    v = unpack_weight(tab_words, tab_scales, "e4m3")[:, unstriped(offs)]
    v2 = unpack_weight(tab2_words, tab2_scales, "e4m3")[:, unstriped(offs2)]
    v3 = unpack_weight(tab3_words, tab3_scales, "e4m3")[:, unstriped(offs3)]
    a = mxq(f64(wa), 0, "e4m3").T @ v
    b = unpack_weight(wb_words, wb_scales, "e2m1").T @ v2
    d = mxq(f64(wd), 0, "e4m3").T @ v3
    lead = np.maximum(b[:, unstriped(pos2)], d[:, unstriped(pos3)])
    z = np.tanh(a[:, unstriped(pos1)]) * lead
    y = unpack_weight(wo_words, wo_scales, "e4m3").T @ mxq(z, 0, "e4m3")
    return y + f64(style)[:, None]

@@ -1,0 +1,237 @@
+from contextlib import ExitStack
+
+import concourse.mybir as mybir
+
+K, M, T, S, CUES, H, N = 1024, 512, 4096, 1024, 512, 1024, 512
+FLOPS = 2 * (K * H * S + 2 * M * H * S + H * N * CUES)
+
+F32 = mybir.dt.float32
+BF16 = mybir.dt.bfloat16
+I32 = mybir.dt.int32
+U32 = mybir.dt.uint32
+U16 = mybir.dt.uint16
+U8 = mybir.dt.uint8
+FP8X4 = mybir.dt.float8_e4m3fn_x4
+FP4X4 = mybir.dt.float4_e2m1fn_x4
+ALU = mybir.AluOpType
+ACT = mybir.ActivationFunctionType
+
+P = 128
+PACK = 4
+KP = P * PACK
+BANK = 512
+
+
+def tile_list_firework_cue_features_kernel(
+    tc, tab_words, tab_scales, tab2_words, tab2_scales, tab3_words, tab3_scales, offs, offs2, offs3,
+    pos1, pos2, pos3, wa, wb_words, wb_scales, wd, wo_words, wo_scales, style, out,
+):
+    nc = tc.nc
+    with ExitStack() as ctx:
+        keep = ctx.enter_context(tc.tile_pool(name="keep", bufs=1))
+        grouped_pool = ctx.enter_context(tc.tile_pool(name="grouped", bufs=4))
+        windows = ctx.enter_context(tc.tile_pool(name="windows", bufs=6))
+        psum1 = ctx.enter_context(tc.psum_pool(name="psum1", bufs=4))
+        psum2 = ctx.enter_context(tc.psum_pool(name="psum2", bufs=1))
+
+        def load_list(name, src):
+            tile = keep.tile([P, src.shape[1]], U16, name=name)
+            nc.sync.dma_start(tile[:], src)
+            return tile
+
+        def zeroed_plane(name, width):
+            tile = keep.tile([P, width], U8, name=name, align_bytes=64)
+            nc.vector.memset(tile[:].bitcast(I32), 0)
+            return tile
+
+        def load_scale_rows(queue, tile, src, first_row):
+            rows = 4 * src.shape[0]
+            for q in range(4):
+                queue.dma_start(
+                    out=tile[32 * q + first_row : 32 * q + first_row + rows, :].bitcast(I32),
+                    in_=src[:, 4 * q : 4 * q + 4, :].bitcast(I32),
+                )
+
+        def held(name, shape, dtype, slot):
+            return keep.tile(shape, dtype, name=name, tag=slot, align_bytes=64)
+
+        def load_table(name, src, a):
+            tile = held(name, [P, T], U32, name)
+            nc.sync.dma_start(out=tile[:].bitcast(I32), in_=src[a].rearrange("p t i -> p (t i)").bitcast(I32))
+            return tile
+
+        def load_weight(name, src, a, b):
+            raw = held(name, [P, PACK, KP], F32, name)
+            rows = src[KP * a : KP * (a + 1), KP * b : KP * (b + 1)]
+            nc.sync.dma_start(out=raw[:], in_=rows.rearrange("(p j) c -> p j c", j=PACK))
+            return raw
+
+        def round_weight(raw):
+            grouped = grouped_pool.tile([P, KP * PACK], BF16, name="grouped", align_bytes=64)
+            nc.scalar.copy(
+                out=grouped[:].rearrange("p (t m j) -> p m t j", t=PACK, j=PACK),
+                in_=raw[:].rearrange("p j (m t) -> p m t j", t=PACK),
+            )
+            return grouped[:]
+
+        def quantise(name, grouped, codes=None):
+            if codes is None:
+                codes = keep.tile([P, KP], U32, name=name + "_codes", align_bytes=64)[:]
+            plane = keep.tile([P, KP], U8, name=name + "_plane", align_bytes=64)
+            nc.vector.quantize_mx(out=codes.bitcast(FP8X4), scales=plane[:], in_=grouped)
+            return codes, plane
+
+        def gather_scales(name, window, offsets, slot):
+            plane = held(name, [P, S], U8, slot)
+            nc.vector.tensor_copy(out=plane[:], in_=window[:].indirect(offsets[:]))
+            return plane
+
+        def gather_words(name, table, offsets):
+            halves = []
+            for h in range(2):
+                words = keep.tile([P, BANK], U32, name=name + str(h), align_bytes=64)
+                nc.vector.tensor_copy(out=words[:], in_=table[:].indirect(offsets[:, 32 * h : 32 * (h + 1)]))
+                halves.append(words)
+            return halves
+
+        def first_stage(passes, slot=None):
+            if slot is None:
+                window = windows.tile([P, S], F32, name="window")
+            else:
+                window = held("window_" + slot, [P, S], F32, slot)
+            for h in range(2):
+                acc = psum1.tile([P, BANK], F32, name="acc")
+                for i, (lhsT, lhsT_scale, halves, plane, row) in enumerate(passes):
+                    nc.tensor.matmul_mx(
+                        out=acc[:], lhsT=lhsT, lhsT_scale=lhsT_scale,
+                        rhs=halves[h][:].bitcast(FP8X4), rhs_scale=plane[row:P, BANK * h : BANK * (h + 1)],
+                        start=(i == 0), stop=(i == len(passes) - 1),
+                    )
+                nc.scalar.copy(out=window[:, BANK * h : BANK * (h + 1)], in_=acc[:])
+            return window
+
+        def stationary(quantised, t):
+            codes, plane = quantised
+            return codes[:, P * t : P * (t + 1)].bitcast(FP8X4), plane[:, P * t : P * (t + 1)]
+
+        s2_window = zeroed_plane("s2_window", T)
+        s3_window = zeroed_plane("s3_window", T)
+        wb_scale_raw = zeroed_plane("wb_scale_raw", H)
+        s1_window = zeroed_plane("s1_window", T)
+        wo_plane = zeroed_plane("wo_plane", N)
+
+        offs2_t = load_list("offs2_t", offs2)
+        offs3_t = load_list("offs3_t", offs3)
+        wb_raw = keep.tile([P, 2 * H], U8, name="wb_raw", align_bytes=64)
+        nc.sync.dma_start(out=wb_raw[:].bitcast(I32), in_=wb_words[0].bitcast(I32))
+        offs_t = load_list("offs_t", offs)
+        load_scale_rows(nc.sync, s2_window, tab2_scales, 0)
+        load_scale_rows(nc.sync, s3_window, tab3_scales, 4)
+        table2 = load_table("table2", tab2_words, 0)
+        load_scale_rows(nc.sync, wb_scale_raw, wb_scales, 0)
+        load_scale_rows(nc.sync, s1_window, tab_scales, 8)
+        pos2_t = load_list("pos2_t", pos2)
+        table3 = load_table("table3", tab3_words, 0)
+        wd_raw = [load_weight("wd_raw" + str(b), wd, 0, b) for b in range(2)]
+        pos3_t = load_list("pos3_t", pos3)
+        pos1_t = load_list("pos1_t", pos1)
+        wa_raw = {}
+        for a in range(2):
+            wa_raw[a, 0] = load_weight("wa_raw%d0" % a, wa, a, 0)
+        table1 = [load_table("table1" + str(a), tab_words, a) for a in range(2)]
+        for a in range(2):
+            wa_raw[a, 1] = load_weight("wa_raw%d1" % a, wa, a, 1)
+        load_scale_rows(nc.sync, wo_plane, wo_scales, 0)
+        wo_codes = keep.tile([P, 2, N], U32, name="wo_codes", align_bytes=64)
+        nc.sync.dma_start(out=wo_codes[:].bitcast(I32), in_=wo_words.rearrange("a p c i -> p a (c i)").bitcast(I32))
+        style_t = keep.tile([P, N // P], F32, name="style_t")
+        with nc.allow_non_contiguous_dma(reason="one value of style for each partition"):
+            nc.sync.dma_start(out=style_t[:], in_=style.rearrange("(c p) -> p c", p=P))
+
+        wb_codes = keep.tile([P, 2 * H], U8, name="wb_codes", align_bytes=64)
+        nc.scalar.copy(
+            out=wb_codes[:].bitcast(U16).rearrange("p (t m) -> p t m", t=PACK),
+            in_=wb_raw[:].bitcast(U16).rearrange("p (m t) -> p t m", t=PACK),
+        )
+        plane2 = gather_scales("plane2", s2_window, offs2_t, "plane2")
+        plane3 = gather_scales("plane3", s3_window, offs3_t, "plane3")
+        wb_plane = keep.tile([P, H], U8, name="wb_plane", align_bytes=64)
+        nc.vector.tensor_copy(
+            out=wb_plane[:].rearrange("p (t m) -> p t m", t=PACK),
+            in_=wb_scale_raw[:].rearrange("p (m t) -> p t m", t=PACK),
+        )
+        words2 = gather_words("words2_", table2, offs2_t)
+        plane1 = gather_scales("plane1", s1_window, offs_t, "table2")
+
+        lead = [held("lead0", [P, PACK, CUES], F32, "lead0")]
+        wd_q = []
+        for b in range(2):
+            for t in range(PACK):
+                c0 = t * (H // PACK) + b * P
+                window = first_stage([(
+                    wb_codes[:, 2 * c0 : 2 * (c0 + P)].bitcast(FP4X4), wb_plane[:, c0 : c0 + P], words2, plane2, 0,
+                )], "wd_raw0" if (b, t) == (1, 1) else None)
+                nc.vector.tensor_copy(out=lead[b][:, t, :], in_=window[:].indirect(pos2_t[:]))
+                if (b, t) == (0, 3):
+                    words3 = gather_words("words3_", table3, offs3_t)
+                    lead.append(held("lead1", [P, PACK, CUES], F32, "table3"))
+                if (b, t) == (1, 0):
+                    wd_q.append(quantise("wd0", round_weight(wd_raw[0])))
+
+        wa_codes = held("wa_codes", [P, 4 * KP], U32, "late")
+        wa_q = {}
+        for b in range(2):
+            picked = held("picked_d" + str(b), [P, PACK, CUES], F32, ("picked_d0", "table11")[b])
+            for t in range(PACK):
+                window = first_stage([stationary(wd_q[b], t) + (words3, plane3, 4)], "wa_raw10" if (b, t) == (1, 0) else None)
+                nc.vector.tensor_copy(out=picked[:, t, :], in_=window[:].indirect(pos3_t[:]))
+            if b == 0:
+                wd_q.append(quantise("wd1", round_weight(wd_raw[1])))
+            nc.vector.tensor_tensor(out=lead[b][:], in0=lead[b][:], in1=picked[:], op=ALU.max)
+            if b == 0:
+                words1 = [gather_words("words1_" + str(a), table1[a], offs_t) for a in range(2)]
+            for a in range(2):
+                i = 2 * b + a
+                wa_q[a, b] = quantise("wa%d%d" % (a, b), round_weight(wa_raw[a, b]), wa_codes[:, KP * i : KP * (i + 1)])
+
+        result = [psum2.tile([P, CUES], F32, name="result" + str(c)) for c in range(N // P)]
+        picked_a = []
+        for b in range(2):
+            picked = held("picked_a" + str(b), [P, PACK, CUES], F32, ("table10", "wd_raw1")[b])
+            picked_a.append(picked)
+            for t in range(PACK):
+                window = first_stage(
+                    [stationary(wa_q[a, b], t) + (words1[a], plane1, 8 + 4 * a) for a in range(2)],
+                    "wa_raw11" if (b, t) == (0, 0) else None,
+                )
+                nc.vector.tensor_copy(out=picked[:, t, :], in_=window[:].indirect(pos1_t[:]))
+        z_both = held("z_both", [P, 2 * KP * PACK], BF16, "wa_raw01")
+        for b in range(2):
+            if b == 0:
+                bounded = held("bounded", [P, PACK, CUES], F32, "late")
+            else:
+                bounded = picked_a[b]
+            nc.scalar.activation(out=bounded[:], in_=picked_a[b][:], func=ACT.Tanh)
+            z = z_both[:, KP * PACK * b : KP * PACK * (b + 1)]
+            nc.vector.tensor_tensor(
+                out=z.rearrange("p (c e t) -> p c t e", t=PACK, e=2),
+                in0=bounded[:].rearrange("p t (c e) -> p c t e", e=2),
+                in1=lead[b][:].rearrange("p t (c e) -> p c t e", e=2),
+                op=ALU.mult,
+            )
+            z_codes, z_plane = quantise("z" + str(b), z)
+            for c in range(N // P):
+                nc.tensor.matmul_mx(
+                    out=result[c][:], lhsT=wo_codes[:, b, P * c : P * (c + 1)].bitcast(FP8X4),
+                    lhsT_scale=wo_plane[4 * b : P, P * c : P * (c + 1)],
+                    rhs=z_codes.bitcast(FP8X4), rhs_scale=z_plane[:],
+                    start=(b == 0), stop=(b == 1),
+                )
+        staged_all = held("staged_all", [P, PACK, KP], F32, "wa_raw00")
+        for c in range(N // P):
+            staged = staged_all[:, c, :]
+            if c % 2 == 0:
+                nc.vector.tensor_scalar(out=staged, in0=result[c][:], scalar1=style_t[:, c : c + 1], scalar2=None, op0=ALU.add)
+            else:
+                nc.scalar.activation(out=staged, in_=result[c][:], func=ACT.Identity, bias=style_t[:, c : c + 1])
+            nc.sync.dma_start(out=out[P * c : P * (c + 1), :], in_=staged)

@@ -69,8 +69,8 @@ def tile_list_firework_cue_features_kernel(
         def round_weight(raw):
             grouped = grouped_pool.tile([P, KP * PACK], BF16, name="grouped", align_bytes=64)
             nc.scalar.copy(
-                out=grouped[:].rearrange("p (t m j) -> p m t j", t=PACK, j=PACK),
-                in_=raw[:].rearrange("p j (m t) -> p m t j", t=PACK),
+                out=grouped[:].rearrange("p (t m j) -> p m j t", t=PACK, j=PACK),
+                in_=raw[:].rearrange("p j (m t) -> p m j t", t=PACK),
             )
             return grouped[:]
 
@@ -86,13 +86,14 @@ def tile_list_firework_cue_features_kernel(
             nc.vector.tensor_copy(out=plane[:], in_=window[:].indirect(offsets[:]))
             return plane
 
-        def gather_words(name, table, offsets):
-            halves = []
-            for h in range(2):
-                words = keep.tile([P, BANK], U32, name=name + str(h), align_bytes=64)
-                nc.vector.tensor_copy(out=words[:], in_=table[:].indirect(offsets[:, 32 * h : 32 * (h + 1)]))
-                halves.append(words)
-            return halves
+        def gather_words(name, table, offsets, slot, pieces=1):
+            words = held(name, [P, S], U32, slot)
+            n = S // pieces
+            for h in range(pieces):
+                nc.vector.tensor_copy(
+                    out=words[:, n * h : n * (h + 1)], in_=table[:].indirect(offsets[:, n // 16 * h : n // 16 * (h + 1)])
+                )
+            return words
 
         def first_stage(passes, slot=None):
             if slot is None:
@@ -104,10 +105,10 @@ def tile_list_firework_cue_features_kernel(
                 for i, (lhsT, lhsT_scale, halves, plane, row) in enumerate(passes):
                     nc.tensor.matmul_mx(
                         out=acc[:], lhsT=lhsT, lhsT_scale=lhsT_scale,
-                        rhs=halves[h][:].bitcast(FP8X4), rhs_scale=plane[row:P, BANK * h : BANK * (h + 1)],
+                        rhs=halves[:, BANK * h : BANK * (h + 1)].bitcast(FP8X4), rhs_scale=plane[row:P, BANK * h : BANK * (h + 1)],
                         start=(i == 0), stop=(i == len(passes) - 1),
                     )
-                nc.scalar.copy(out=window[:, BANK * h : BANK * (h + 1)], in_=acc[:])
+                nc.scalar.activation(out=window[:, BANK * h : BANK * (h + 1)], in_=acc[:], func=ACT.Copy)
             return window
 
         def stationary(quantised, t):
@@ -124,11 +125,11 @@ def tile_list_firework_cue_features_kernel(
         offs3_t = load_list("offs3_t", offs3)
         wb_raw = keep.tile([P, 2 * H], U8, name="wb_raw", align_bytes=64)
         nc.sync.dma_start(out=wb_raw[:].bitcast(I32), in_=wb_words[0].bitcast(I32))
-        offs_t = load_list("offs_t", offs)
         load_scale_rows(nc.sync, s2_window, tab2_scales, 0)
-        load_scale_rows(nc.sync, s3_window, tab3_scales, 4)
         table2 = load_table("table2", tab2_words, 0)
+        load_scale_rows(nc.sync, s3_window, tab3_scales, 4)
         load_scale_rows(nc.sync, wb_scale_raw, wb_scales, 0)
+        offs_t = load_list("offs_t", offs)
         load_scale_rows(nc.sync, s1_window, tab_scales, 8)
         pos2_t = load_list("pos2_t", pos2)
         table3 = load_table("table3", tab3_words, 0)
@@ -154,13 +155,13 @@ def tile_list_firework_cue_features_kernel(
             in_=wb_raw[:].bitcast(U16).rearrange("p (m t) -> p t m", t=PACK),
         )
         plane2 = gather_scales("plane2", s2_window, offs2_t, "plane2")
+        words2 = gather_words("words2", table2, offs2_t, "words2", 2)
         plane3 = gather_scales("plane3", s3_window, offs3_t, "plane3")
         wb_plane = keep.tile([P, H], U8, name="wb_plane", align_bytes=64)
         nc.vector.tensor_copy(
             out=wb_plane[:].rearrange("p (t m) -> p t m", t=PACK),
             in_=wb_scale_raw[:].rearrange("p (m t) -> p t m", t=PACK),
         )
-        words2 = gather_words("words2_", table2, offs2_t)
         plane1 = gather_scales("plane1", s1_window, offs_t, "table2")
 
         lead = [held("lead0", [P, PACK, CUES], F32, "lead0")]
@@ -170,10 +171,10 @@ def tile_list_firework_cue_features_kernel(
                 c0 = t * (H // PACK) + b * P
                 window = first_stage([(
                     wb_codes[:, 2 * c0 : 2 * (c0 + P)].bitcast(FP4X4), wb_plane[:, c0 : c0 + P], words2, plane2, 0,
-                )], "wd_raw0" if (b, t) == (1, 1) else None)
+                )], {(0, 2): "words3", (1, 1): "wd_raw0"}.get((b, t)))
                 nc.vector.tensor_copy(out=lead[b][:, t, :], in_=window[:].indirect(pos2_t[:]))
                 if (b, t) == (0, 3):
-                    words3 = gather_words("words3_", table3, offs3_t)
+                    words3 = gather_words("words3", table3, offs3_t, "words3")
                     lead.append(held("lead1", [P, PACK, CUES], F32, "table3"))
                 if (b, t) == (1, 0):
                     wd_q.append(quantise("wd0", round_weight(wd_raw[0])))
@@ -189,12 +190,11 @@ def tile_list_firework_cue_features_kernel(
                 wd_q.append(quantise("wd1", round_weight(wd_raw[1])))
             nc.vector.tensor_tensor(out=lead[b][:], in0=lead[b][:], in1=picked[:], op=ALU.max)
             if b == 0:
-                words1 = [gather_words("words1_" + str(a), table1[a], offs_t) for a in range(2)]
+                words1 = [gather_words("words1" + str(a), table1[a], offs_t, "words1" + str(a)) for a in range(2)]
             for a in range(2):
                 i = 2 * b + a
                 wa_q[a, b] = quantise("wa%d%d" % (a, b), round_weight(wa_raw[a, b]), wa_codes[:, KP * i : KP * (i + 1)])
 
-        result = [psum2.tile([P, CUES], F32, name="result" + str(c)) for c in range(N // P)]
         picked_a = []
         for b in range(2):
             picked = held("picked_a" + str(b), [P, PACK, CUES], F32, ("table10", "wd_raw1")[b])
@@ -206,6 +206,10 @@ def tile_list_firework_cue_features_kernel(
                 )
                 nc.vector.tensor_copy(out=picked[:, t, :], in_=window[:].indirect(pos1_t[:]))
         z_both = held("z_both", [P, 2 * KP * PACK], BF16, "wa_raw01")
+        half = CUES // 2
+        result = [[psum2.tile([P, half], F32, name="result" + str(c)) for c in range(N // P)]]
+        result.append([psum1.tile([P, half], F32, name="acc") for c in range(N // P)])
+        staged_all = held("staged_all", [P, PACK, KP], F32, "wa_raw00")
         for b in range(2):
             if b == 0:
                 bounded = held("bounded", [P, PACK, CUES], F32, "late")
@@ -213,25 +217,36 @@ def tile_list_firework_cue_features_kernel(
                 bounded = picked_a[b]
             nc.scalar.activation(out=bounded[:], in_=picked_a[b][:], func=ACT.Tanh)
             z = z_both[:, KP * PACK * b : KP * PACK * (b + 1)]
-            nc.vector.tensor_tensor(
-                out=z.rearrange("p (c e t) -> p c t e", t=PACK, e=2),
-                in0=bounded[:].rearrange("p t (c e) -> p c t e", e=2),
-                in1=lead[b][:].rearrange("p t (c e) -> p c t e", e=2),
-                op=ALU.mult,
-            )
-            z_codes, z_plane = quantise("z" + str(b), z)
-            for c in range(N // P):
-                nc.tensor.matmul_mx(
-                    out=result[c][:], lhsT=wo_codes[:, b, P * c : P * (c + 1)].bitcast(FP8X4),
-                    lhsT_scale=wo_plane[4 * b : P, P * c : P * (c + 1)],
-                    rhs=z_codes.bitcast(FP8X4), rhs_scale=z_plane[:],
-                    start=(b == 0), stop=(b == 1),
+            z_codes = keep.tile([P, CUES], U32, name="z_codes" + str(b), align_bytes=64)
+            z_plane = keep.tile([P, CUES], U8, name="z_plane" + str(b), align_bytes=64)
+            pieces = b + 1
+            n = CUES // pieces
+            for h in range(pieces):
+                nc.vector.tensor_tensor(
+                    out=z[:, PACK * n * h : PACK * n * (h + 1)].rearrange("p (c e t) -> p c t e", t=PACK, e=2),
+                    in0=bounded[:, :, n * h : n * (h + 1)].rearrange("p t (c e) -> p c t e", e=2),
+                    in1=lead[b][:, :, n * h : n * (h + 1)].rearrange("p t (c e) -> p c t e", e=2),
+                    op=ALU.mult,
                 )
-        staged_all = held("staged_all", [P, PACK, KP], F32, "wa_raw00")
-        for c in range(N // P):
-            staged = staged_all[:, c, :]
-            if c % 2 == 0:
-                nc.vector.tensor_scalar(out=staged, in0=result[c][:], scalar1=style_t[:, c : c + 1], scalar2=None, op0=ALU.add)
-            else:
-                nc.scalar.activation(out=staged, in_=result[c][:], func=ACT.Identity, bias=style_t[:, c : c + 1])
-            nc.sync.dma_start(out=out[P * c : P * (c + 1), :], in_=staged)
+            for h in range(pieces):
+                nc.vector.quantize_mx(
+                    out=z_codes[:, n * h : n * (h + 1)].bitcast(FP8X4), scales=z_plane[:, n * h : n * (h + 1)],
+                    in_=z[:, PACK * n * h : PACK * n * (h + 1)],
+                )
+            for h in range(2):
+                cols = slice(half * h, half * (h + 1))
+                for c in range(N // P):
+                    nc.tensor.matmul_mx(
+                        out=result[h][c][:], lhsT=wo_codes[:, b, P * c : P * (c + 1)].bitcast(FP8X4),
+                        lhsT_scale=wo_plane[4 * b : P, P * c : P * (c + 1)],
+                        rhs=z_codes[:, cols].bitcast(FP8X4), rhs_scale=z_plane[:, cols],
+                        start=(b == 0), stop=(b == 1),
+                    )
+                    if b == 1:
+                        staged = staged_all[:, c, cols]
+                        bias = style_t[:, c : c + 1]
+                        if h == 1 and c % 2 == 0:
+                            nc.vector.tensor_scalar(out=staged, in0=result[h][c][:], scalar1=bias, scalar2=None, op0=ALU.add)
+                        else:
+                            nc.scalar.activation(out=staged, in_=result[h][c][:], func=ACT.Identity, bias=bias)
+                        nc.sync.dma_start(out=out[P * c : P * (c + 1), cols], in_=staged)

@@ -95,11 +95,11 @@ def tile_list_firework_cue_features_kernel(
                 )
             return words
 
-        def first_stage(passes, slot=None):
-            if slot is None:
-                window = windows.tile([P, S], F32, name="window")
-            else:
-                window = held("window_" + slot, [P, S], F32, slot)
+        def first_stage(passes, slot=None, window=None):
+            if slot is not None:
+                window = held("window_" + slot, [P, S], F32, slot)[:]
+            elif window is None:
+                window = windows.tile([P, S], F32, name="window")[:]
             for h in range(2):
                 acc = psum1.tile([P, BANK], F32, name="acc")
                 for i, (lhsT, lhsT_scale, halves, plane, row) in enumerate(passes):
@@ -116,8 +116,8 @@ def tile_list_firework_cue_features_kernel(
             return codes[:, P * t : P * (t + 1)].bitcast(FP8X4), plane[:, P * t : P * (t + 1)]
 
         s2_window = zeroed_plane("s2_window", T)
-        s3_window = zeroed_plane("s3_window", T)
         wb_scale_raw = zeroed_plane("wb_scale_raw", H)
+        s3_window = zeroed_plane("s3_window", T)
         s1_window = zeroed_plane("s1_window", T)
         wo_plane = zeroed_plane("wo_plane", N)
 
@@ -127,11 +127,11 @@ def tile_list_firework_cue_features_kernel(
         nc.sync.dma_start(out=wb_raw[:].bitcast(I32), in_=wb_words[0].bitcast(I32))
         load_scale_rows(nc.sync, s2_window, tab2_scales, 0)
         table2 = load_table("table2", tab2_words, 0)
-        load_scale_rows(nc.sync, s3_window, tab3_scales, 4)
         load_scale_rows(nc.sync, wb_scale_raw, wb_scales, 0)
+        load_scale_rows(nc.sync, s3_window, tab3_scales, 4)
+        pos2_t = load_list("pos2_t", pos2)
         offs_t = load_list("offs_t", offs)
         load_scale_rows(nc.sync, s1_window, tab_scales, 8)
-        pos2_t = load_list("pos2_t", pos2)
         table3 = load_table("table3", tab3_words, 0)
         wd_raw = [load_weight("wd_raw" + str(b), wd, 0, b) for b in range(2)]
         pos3_t = load_list("pos3_t", pos3)
@@ -156,12 +156,12 @@ def tile_list_firework_cue_features_kernel(
         )
         plane2 = gather_scales("plane2", s2_window, offs2_t, "plane2")
         words2 = gather_words("words2", table2, offs2_t, "words2", 2)
-        plane3 = gather_scales("plane3", s3_window, offs3_t, "plane3")
         wb_plane = keep.tile([P, H], U8, name="wb_plane", align_bytes=64)
         nc.vector.tensor_copy(
             out=wb_plane[:].rearrange("p (t m) -> p t m", t=PACK),
             in_=wb_scale_raw[:].rearrange("p (m t) -> p t m", t=PACK),
         )
+        plane3 = gather_scales("plane3", s3_window, offs3_t, "plane3")
         plane1 = gather_scales("plane1", s1_window, offs_t, "table2")
 
         lead = [held("lead0", [P, PACK, CUES], F32, "lead0")]
@@ -172,7 +172,7 @@ def tile_list_firework_cue_features_kernel(
                 window = first_stage([(
                     wb_codes[:, 2 * c0 : 2 * (c0 + P)].bitcast(FP4X4), wb_plane[:, c0 : c0 + P], words2, plane2, 0,
                 )], {(0, 2): "words3", (1, 1): "wd_raw0"}.get((b, t)))
-                nc.vector.tensor_copy(out=lead[b][:, t, :], in_=window[:].indirect(pos2_t[:]))
+                nc.vector.tensor_copy(out=lead[b][:, t, :], in_=window.indirect(pos2_t[:]))
                 if (b, t) == (0, 3):
                     words3 = gather_words("words3", table3, offs3_t, "words3")
                     lead.append(held("lead1", [P, PACK, CUES], F32, "table3"))
@@ -184,10 +184,10 @@ def tile_list_firework_cue_features_kernel(
         for b in range(2):
             picked = held("picked_d" + str(b), [P, PACK, CUES], F32, ("picked_d0", "table11")[b])
             for t in range(PACK):
-                window = first_stage([stationary(wd_q[b], t) + (words3, plane3, 4)], "wa_raw10" if (b, t) == (1, 0) else None)
-                nc.vector.tensor_copy(out=picked[:, t, :], in_=window[:].indirect(pos3_t[:]))
-            if b == 0:
-                wd_q.append(quantise("wd1", round_weight(wd_raw[1])))
+                window = first_stage([stationary(wd_q[b], t) + (words3, plane3, 4)], {(0, 3): "wd_raw1", (1, 0): "wa_raw10"}.get((b, t)))
+                nc.vector.tensor_copy(out=picked[:, t, :], in_=window.indirect(pos3_t[:]))
+                if (b, t) == (0, 2):
+                    wd_q.append(quantise("wd1", round_weight(wd_raw[1])))
             nc.vector.tensor_tensor(out=lead[b][:], in0=lead[b][:], in1=picked[:], op=ALU.max)
             if b == 0:
                 words1 = [gather_words("words1" + str(a), table1[a], offs_t, "words1" + str(a)) for a in range(2)]
@@ -196,15 +196,16 @@ def tile_list_firework_cue_features_kernel(
                 wa_q[a, b] = quantise("wa%d%d" % (a, b), round_weight(wa_raw[a, b]), wa_codes[:, KP * i : KP * (i + 1)])
 
         picked_a = []
+        pair = held("window_pair", [P, 2 * S], F32, "wa_raw11")
         for b in range(2):
             picked = held("picked_a" + str(b), [P, PACK, CUES], F32, ("table10", "wd_raw1")[b])
             picked_a.append(picked)
             for t in range(PACK):
                 window = first_stage(
                     [stationary(wa_q[a, b], t) + (words1[a], plane1, 8 + 4 * a) for a in range(2)],
-                    "wa_raw11" if (b, t) == (0, 0) else None,
+                    window=pair[:, S * t : S * (t + 1)] if b == 0 and t < 2 else None,
                 )
-                nc.vector.tensor_copy(out=picked[:, t, :], in_=window[:].indirect(pos1_t[:]))
+                nc.vector.tensor_copy(out=picked[:, t, :], in_=window.indirect(pos1_t[:]))
         z_both = held("z_both", [P, 2 * KP * PACK], BF16, "wa_raw01")
         half = CUES // 2
         result = [[psum2.tile([P, half], F32, name="result" + str(c)) for c in range(N // P)]]
@@ -228,7 +229,6 @@ def tile_list_firework_cue_features_kernel(
                     in1=lead[b][:, :, n * h : n * (h + 1)].rearrange("p t (c e) -> p c t e", e=2),
                     op=ALU.mult,
                 )
-            for h in range(pieces):
                 nc.vector.quantize_mx(
                     out=z_codes[:, n * h : n * (h + 1)].bitcast(FP8X4), scales=z_plane[:, n * h : n * (h + 1)],
                     in_=z[:, PACK * n * h : PACK * n * (h + 1)],

@@ -171,15 +171,14 @@ def tile_list_firework_cue_features_kernel(
                 c0 = t * (H // PACK) + b * P
                 window = first_stage([(
                     wb_codes[:, 2 * c0 : 2 * (c0 + P)].bitcast(FP4X4), wb_plane[:, c0 : c0 + P], words2, plane2, 0,
-                )], {(0, 2): "words3", (1, 1): "wd_raw0"}.get((b, t)))
+                )], {(0, 2): "words3", (1, 0): "wd_raw0"}.get((b, t)))
                 nc.vector.tensor_copy(out=lead[b][:, t, :], in_=window.indirect(pos2_t[:]))
                 if (b, t) == (0, 3):
                     words3 = gather_words("words3", table3, offs3_t, "words3")
                     lead.append(held("lead1", [P, PACK, CUES], F32, "table3"))
-                if (b, t) == (1, 0):
                     wd_q.append(quantise("wd0", round_weight(wd_raw[0])))
 
-        wa_codes = held("wa_codes", [P, 4 * KP], U32, "late")
+        wa_codes = held("wa_codes", [P, 4 * KP], U32, "table10")
         wa_q = {}
         for b in range(2):
             picked = held("picked_d" + str(b), [P, PACK, CUES], F32, ("picked_d0", "table11")[b])
@@ -198,7 +197,7 @@ def tile_list_firework_cue_features_kernel(
         picked_a = []
         pair = held("window_pair", [P, 2 * S], F32, "wa_raw11")
         for b in range(2):
-            picked = held("picked_a" + str(b), [P, PACK, CUES], F32, ("table10", "wd_raw1")[b])
+            picked = held("picked_a" + str(b), [P, PACK, CUES], F32, ("picked_a0", "wd_raw1")[b])
             picked_a.append(picked)
             for t in range(PACK):
                 window = first_stage(
@@ -213,7 +212,7 @@ def tile_list_firework_cue_features_kernel(
         staged_all = held("staged_all", [P, PACK, KP], F32, "wa_raw00")
         for b in range(2):
             if b == 0:
-                bounded = held("bounded", [P, PACK, CUES], F32, "late")
+                bounded = held("bounded", [P, PACK, CUES], F32, "table10")
             else:
                 bounded = picked_a[b]
             nc.scalar.activation(out=bounded[:], in_=picked_a[b][:], func=ACT.Tanh)

from contextlib import ExitStack

import concourse.mybir as mybir

K, M, T, S, CUES, H, N = 1024, 512, 4096, 1024, 512, 1024, 512
FLOPS = 2 * (K * H * S + 2 * M * H * S + H * N * CUES)

F32 = mybir.dt.float32
BF16 = mybir.dt.bfloat16
I32 = mybir.dt.int32
U32 = mybir.dt.uint32
U16 = mybir.dt.uint16
U8 = mybir.dt.uint8
FP8X4 = mybir.dt.float8_e4m3fn_x4
FP4X4 = mybir.dt.float4_e2m1fn_x4
ALU = mybir.AluOpType
ACT = mybir.ActivationFunctionType

P = 128
PACK = 4
KP = P * PACK
BANK = 512


def tile_list_firework_cue_features_kernel(
    tc, tab_words, tab_scales, tab2_words, tab2_scales, tab3_words, tab3_scales, offs, offs2, offs3,
    pos1, pos2, pos3, wa, wb_words, wb_scales, wd, wo_words, wo_scales, style, out,
):
    nc = tc.nc
    with ExitStack() as ctx:
        keep = ctx.enter_context(tc.tile_pool(name="keep", bufs=1))
        grouped_pool = ctx.enter_context(tc.tile_pool(name="grouped", bufs=4))
        windows = ctx.enter_context(tc.tile_pool(name="windows", bufs=6))
        psum1 = ctx.enter_context(tc.psum_pool(name="psum1", bufs=4))
        psum2 = ctx.enter_context(tc.psum_pool(name="psum2", bufs=1))

        def load_list(name, src):
            tile = keep.tile([P, src.shape[1]], U16, name=name)
            nc.sync.dma_start(tile[:], src)
            return tile

        def zeroed_plane(name, width):
            tile = keep.tile([P, width], U8, name=name, align_bytes=64)
            nc.vector.memset(tile[:].bitcast(I32), 0)
            return tile

        def load_scale_rows(queue, tile, src, first_row):
            rows = 4 * src.shape[0]
            for q in range(4):
                queue.dma_start(
                    out=tile[32 * q + first_row : 32 * q + first_row + rows, :].bitcast(I32),
                    in_=src[:, 4 * q : 4 * q + 4, :].bitcast(I32),
                )

        def held(name, shape, dtype, slot):
            return keep.tile(shape, dtype, name=name, tag=slot, align_bytes=64)

        def load_table(name, src, a):
            tile = held(name, [P, T], U32, name)
            nc.sync.dma_start(out=tile[:].bitcast(I32), in_=src[a].rearrange("p t i -> p (t i)").bitcast(I32))
            return tile

        def load_weight(name, src, a, b):
            raw = held(name, [P, PACK, KP], F32, name)
            rows = src[KP * a : KP * (a + 1), KP * b : KP * (b + 1)]
            nc.sync.dma_start(out=raw[:], in_=rows.rearrange("(p j) c -> p j c", j=PACK))
            return raw

        def round_weight(raw):
            grouped = grouped_pool.tile([P, KP * PACK], BF16, name="grouped", align_bytes=64)
            nc.scalar.copy(
                out=grouped[:].rearrange("p (t m j) -> p m j t", t=PACK, j=PACK),
                in_=raw[:].rearrange("p j (m t) -> p m j t", t=PACK),
            )
            return grouped[:]

        def quantise(name, grouped, codes=None):
            if codes is None:
                codes = keep.tile([P, KP], U32, name=name + "_codes", align_bytes=64)[:]
            plane = keep.tile([P, KP], U8, name=name + "_plane", align_bytes=64)
            nc.vector.quantize_mx(out=codes.bitcast(FP8X4), scales=plane[:], in_=grouped)
            return codes, plane

        def gather_scales(name, window, offsets, slot):
            plane = held(name, [P, S], U8, slot)
            nc.vector.tensor_copy(out=plane[:], in_=window[:].indirect(offsets[:]))
            return plane

        def gather_words(name, table, offsets, slot, pieces=1):
            words = held(name, [P, S], U32, slot)
            n = S // pieces
            for h in range(pieces):
                nc.vector.tensor_copy(
                    out=words[:, n * h : n * (h + 1)], in_=table[:].indirect(offsets[:, n // 16 * h : n // 16 * (h + 1)])
                )
            return words

        def first_stage(passes, slot=None, window=None):
            if slot is not None:
                window = held("window_" + slot, [P, S], F32, slot)[:]
            elif window is None:
                window = windows.tile([P, S], F32, name="window")[:]
            for h in range(2):
                acc = psum1.tile([P, BANK], F32, name="acc")
                for i, (lhsT, lhsT_scale, halves, plane, row) in enumerate(passes):
                    nc.tensor.matmul_mx(
                        out=acc[:], lhsT=lhsT, lhsT_scale=lhsT_scale,
                        rhs=halves[:, BANK * h : BANK * (h + 1)].bitcast(FP8X4), rhs_scale=plane[row:P, BANK * h : BANK * (h + 1)],
                        start=(i == 0), stop=(i == len(passes) - 1),
                    )
                nc.scalar.activation(out=window[:, BANK * h : BANK * (h + 1)], in_=acc[:], func=ACT.Copy)
            return window

        def stationary(quantised, t):
            codes, plane = quantised
            return codes[:, P * t : P * (t + 1)].bitcast(FP8X4), plane[:, P * t : P * (t + 1)]

        s2_window = zeroed_plane("s2_window", T)
        wb_scale_raw = zeroed_plane("wb_scale_raw", H)
        s3_window = zeroed_plane("s3_window", T)
        s1_window = zeroed_plane("s1_window", T)
        wo_plane = zeroed_plane("wo_plane", N)

        offs2_t = load_list("offs2_t", offs2)
        offs3_t = load_list("offs3_t", offs3)
        wb_raw = keep.tile([P, 2 * H], U8, name="wb_raw", align_bytes=64)
        nc.sync.dma_start(out=wb_raw[:].bitcast(I32), in_=wb_words[0].bitcast(I32))
        load_scale_rows(nc.sync, s2_window, tab2_scales, 0)
        table2 = load_table("table2", tab2_words, 0)
        load_scale_rows(nc.sync, wb_scale_raw, wb_scales, 0)
        load_scale_rows(nc.sync, s3_window, tab3_scales, 4)
        pos2_t = load_list("pos2_t", pos2)
        offs_t = load_list("offs_t", offs)
        load_scale_rows(nc.sync, s1_window, tab_scales, 8)
        table3 = load_table("table3", tab3_words, 0)
        wd_raw = [load_weight("wd_raw" + str(b), wd, 0, b) for b in range(2)]
        pos3_t = load_list("pos3_t", pos3)
        pos1_t = load_list("pos1_t", pos1)
        wa_raw = {}
        for a in range(2):
            wa_raw[a, 0] = load_weight("wa_raw%d0" % a, wa, a, 0)
        table1 = [load_table("table1" + str(a), tab_words, a) for a in range(2)]
        for a in range(2):
            wa_raw[a, 1] = load_weight("wa_raw%d1" % a, wa, a, 1)
        load_scale_rows(nc.sync, wo_plane, wo_scales, 0)
        wo_codes = keep.tile([P, 2, N], U32, name="wo_codes", align_bytes=64)
        nc.sync.dma_start(out=wo_codes[:].bitcast(I32), in_=wo_words.rearrange("a p c i -> p a (c i)").bitcast(I32))
        style_t = keep.tile([P, N // P], F32, name="style_t")
        with nc.allow_non_contiguous_dma(reason="one value of style for each partition"):
            nc.sync.dma_start(out=style_t[:], in_=style.rearrange("(c p) -> p c", p=P))

        wb_codes = keep.tile([P, 2 * H], U8, name="wb_codes", align_bytes=64)
        nc.scalar.copy(
            out=wb_codes[:].bitcast(U16).rearrange("p (t m) -> p t m", t=PACK),
            in_=wb_raw[:].bitcast(U16).rearrange("p (m t) -> p t m", t=PACK),
        )
        plane2 = gather_scales("plane2", s2_window, offs2_t, "plane2")
        words2 = gather_words("words2", table2, offs2_t, "words2", 2)
        wb_plane = keep.tile([P, H], U8, name="wb_plane", align_bytes=64)
        nc.vector.tensor_copy(
            out=wb_plane[:].rearrange("p (t m) -> p t m", t=PACK),
            in_=wb_scale_raw[:].rearrange("p (m t) -> p t m", t=PACK),
        )
        plane3 = gather_scales("plane3", s3_window, offs3_t, "plane3")
        plane1 = gather_scales("plane1", s1_window, offs_t, "table2")

        lead = [held("lead0", [P, PACK, CUES], F32, "lead0")]
        wd_q = []
        for b in range(2):
            for t in range(PACK):
                c0 = t * (H // PACK) + b * P
                window = first_stage([(
                    wb_codes[:, 2 * c0 : 2 * (c0 + P)].bitcast(FP4X4), wb_plane[:, c0 : c0 + P], words2, plane2, 0,
                )], {(0, 2): "words3", (1, 0): "wd_raw0"}.get((b, t)))
                nc.vector.tensor_copy(out=lead[b][:, t, :], in_=window.indirect(pos2_t[:]))
                if (b, t) == (0, 3):
                    words3 = gather_words("words3", table3, offs3_t, "words3")
                    lead.append(held("lead1", [P, PACK, CUES], F32, "table3"))
                    wd_q.append(quantise("wd0", round_weight(wd_raw[0])))

        wa_codes = held("wa_codes", [P, 4 * KP], U32, "table10")
        wa_q = {}
        for b in range(2):
            picked = held("picked_d" + str(b), [P, PACK, CUES], F32, ("picked_d0", "table11")[b])
            for t in range(PACK):
                window = first_stage([stationary(wd_q[b], t) + (words3, plane3, 4)], {(0, 3): "wd_raw1", (1, 0): "wa_raw10"}.get((b, t)))
                nc.vector.tensor_copy(out=picked[:, t, :], in_=window.indirect(pos3_t[:]))
                if (b, t) == (0, 2):
                    wd_q.append(quantise("wd1", round_weight(wd_raw[1])))
            nc.vector.tensor_tensor(out=lead[b][:], in0=lead[b][:], in1=picked[:], op=ALU.max)
            if b == 0:
                words1 = [gather_words("words1" + str(a), table1[a], offs_t, "words1" + str(a)) for a in range(2)]
            for a in range(2):
                i = 2 * b + a
                wa_q[a, b] = quantise("wa%d%d" % (a, b), round_weight(wa_raw[a, b]), wa_codes[:, KP * i : KP * (i + 1)])

        picked_a = []
        pair = held("window_pair", [P, 2 * S], F32, "wa_raw11")
        for b in range(2):
            picked = held("picked_a" + str(b), [P, PACK, CUES], F32, ("picked_a0", "wd_raw1")[b])
            picked_a.append(picked)
            for t in range(PACK):
                window = first_stage(
                    [stationary(wa_q[a, b], t) + (words1[a], plane1, 8 + 4 * a) for a in range(2)],
                    window=pair[:, S * t : S * (t + 1)] if b == 0 and t < 2 else None,
                )
                nc.vector.tensor_copy(out=picked[:, t, :], in_=window.indirect(pos1_t[:]))
        z_both = held("z_both", [P, 2 * KP * PACK], BF16, "wa_raw01")
        half = CUES // 2
        result = [[psum2.tile([P, half], F32, name="result" + str(c)) for c in range(N // P)]]
        result.append([psum1.tile([P, half], F32, name="acc") for c in range(N // P)])
        staged_all = held("staged_all", [P, PACK, KP], F32, "wa_raw00")
        for b in range(2):
            if b == 0:
                bounded = held("bounded", [P, PACK, CUES], F32, "table10")
            else:
                bounded = picked_a[b]
            nc.scalar.activation(out=bounded[:], in_=picked_a[b][:], func=ACT.Tanh)
            z = z_both[:, KP * PACK * b : KP * PACK * (b + 1)]
            z_codes = keep.tile([P, CUES], U32, name="z_codes" + str(b), align_bytes=64)
            z_plane = keep.tile([P, CUES], U8, name="z_plane" + str(b), align_bytes=64)
            pieces = b + 1
            n = CUES // pieces
            for h in range(pieces):
                nc.vector.tensor_tensor(
                    out=z[:, PACK * n * h : PACK * n * (h + 1)].rearrange("p (c e t) -> p c t e", t=PACK, e=2),
                    in0=bounded[:, :, n * h : n * (h + 1)].rearrange("p t (c e) -> p c t e", e=2),
                    in1=lead[b][:, :, n * h : n * (h + 1)].rearrange("p t (c e) -> p c t e", e=2),
                    op=ALU.mult,
                )
                nc.vector.quantize_mx(
                    out=z_codes[:, n * h : n * (h + 1)].bitcast(FP8X4), scales=z_plane[:, n * h : n * (h + 1)],
                    in_=z[:, PACK * n * h : PACK * n * (h + 1)],
                )
            for h in range(2):
                cols = slice(half * h, half * (h + 1))
                for c in range(N // P):
                    nc.tensor.matmul_mx(
                        out=result[h][c][:], lhsT=wo_codes[:, b, P * c : P * (c + 1)].bitcast(FP8X4),
                        lhsT_scale=wo_plane[4 * b : P, P * c : P * (c + 1)],
                        rhs=z_codes[:, cols].bitcast(FP8X4), rhs_scale=z_plane[:, cols],
                        start=(b == 0), stop=(b == 1),
                    )
                    if b == 1:
                        staged = staged_all[:, c, cols]
                        bias = style_t[:, c : c + 1]
                        if h == 1 and c % 2 == 0:
                            nc.vector.tensor_scalar(out=staged, in0=result[h][c][:], scalar1=bias, scalar2=None, op0=ALU.add)
                        else:
                            nc.scalar.activation(out=staged, in_=result[h][c][:], func=ACT.Identity, bias=bias)
                        nc.sync.dma_start(out=out[P * c : P * (c + 1), cols], in_=staged)
